import numpy as np
import ml_dtypes


def mxq(x, axis, fmt="e4m3"):
    dtype, down = {"e4m3": (ml_dtypes.float8_e4m3fn, 7), "e5m2": (ml_dtypes.float8_e5m2, 14)}[fmt]
    v = np.moveaxis(np.asarray(x, np.float32).astype(ml_dtypes.bfloat16).astype(np.float64), axis, -1)
    blocks = v.reshape(v.shape[:-1] + (-1, 32))
    amax = np.abs(blocks).max(-1, keepdims=True)
    byte = np.maximum(np.where(amax > 0, np.frexp(amax)[1] - 1 + 127, 0) - down, 1)
    scale = np.exp2(byte - 127.0)
    codes = (blocks / scale).astype(np.float32).astype(dtype).astype(np.float64)
    return np.moveaxis((codes * scale).reshape(v.shape), -1, axis)


WIDE = False


def mx_kscale(k):
    if not WIDE:
        return np.ones(k)
    levels = np.array([10, -10, 5, -5, 0])
    if k % 512:
        return np.exp2(np.random.permutation(np.resize(levels, k // 32))).repeat(32)
    a = np.empty((k // 512, 16))
    for p in range(k // 512):
        a[p, :8] = np.random.permutation(np.resize(levels, 8))
        for g in range(8):
            far = levels[np.abs(levels - a[p, g]) >= 10]
            a[p, g + 8] = far[np.random.randint(len(far))]
    return np.exp2(a.ravel()).repeat(32)


def f64(x):
    return np.asarray(x).astype(np.float64)


def striped(idx):
    return np.tile(idx.reshape(-1, 16).T, (8, 1)).astype(np.uint16)


def unstriped(offs):
    return offs[:16].T.reshape(-1).astype(np.int64)


E2M1 = np.array([0.0, 0.5, 1.0, 1.5, 2.0, 3.0, 4.0, 6.0, -0.0, -0.5, -1.0, -1.5, -2.0, -3.0, -4.0, -6.0])


def pack_weight(w, fmt):
    k, n = w.shape
    w = f64(np.asarray(w, np.float32).astype(ml_dtypes.bfloat16)).reshape(k // 32, 32, n)
    amax = np.abs(w).max(1)
    if fmt == "e4m3":
        byte = np.frexp(amax)[1] - 1 + 127 - 7
    else:
        mant, ex = np.frexp(amax / 6.0)
        byte = np.where(mant > 0.5, ex, ex - 1) + 127
    byte = np.clip(np.where(amax > 0, byte, 1), 1, 254)
    scaled = (w * np.exp2(127.0 - byte)[:, None, :]).reshape(k, n).astype(np.float32)
    by_word = np.ascontiguousarray(scaled.reshape(k // 512, 128, 4, n).transpose(0, 1, 3, 2))
    if fmt == "e4m3":
        words = by_word.astype(ml_dtypes.float8_e4m3fn).view(np.uint8)
    else:
        c = by_word.astype(ml_dtypes.float4_e2m1fn).view(np.uint8) & 0xF
        words = (c[..., 0::2] | (c[..., 1::2] << 4)).reshape(k // 512, 128, 2 * n)
    return np.ascontiguousarray(words), np.ascontiguousarray(byte.astype(np.uint8).reshape(k // 512, 16, n))


def unpack_weight(words, scales, fmt):
    g, _, n = scales.shape
    words = np.ascontiguousarray(words).reshape(g, 128, n, -1)
    if fmt == "e4m3":
        vals = words.view(ml_dtypes.float8_e4m3fn).astype(np.float64)
    else:
        nib = np.empty((g, 128, n, 4), np.uint8)
        nib[..., 0::2] = words & 0xF
        nib[..., 1::2] = words >> 4
        vals = E2M1[nib]
    vals = vals * np.repeat(np.exp2(scales.astype(np.float64) - 127.0), 8, axis=1)[..., None]
    return vals.transpose(0, 1, 3, 2).reshape(g * 512, n)


def pack_table(v):
    words, scales = pack_weight(v, "e4m3")
    return np.concatenate([words.reshape(words.shape[0], -1), scales.reshape(scales.shape[0], -1)], axis=1)


def unpack_table(tab):
    g, t = tab.shape[0], tab.shape[1] // 528
    return unpack_weight(tab[:, :512 * t].reshape(g, 128, t, 4), tab[:, 512 * t:].reshape(g, 16, t), "e4m3")


def silu(v):
    return v / (1.0 + np.exp(-np.maximum(v, -700.0)))


K, M, T, S = 1024, 512, 1024, 512


def setup_inputs():
    n = np.random.standard_normal
    s = mx_kscale(K)[:, None]
    s2 = mx_kscale(512)[:, None]
    p_w4 = pack_weight(n((K, M)) / np.sqrt(K) / s, "e2m1")
    return {
        "tab": pack_table(n((K, T)) * s),
        "w4_words": p_w4[0],
        "w4_scales": p_w4[1],
        "c": (n((512, S)) * s2).astype(np.float32),
        "u": (n((512, M)) / np.sqrt(512) / s2).astype(np.float32),
        "b": (0.3 * n(512)).astype(np.float32),
        "wgo": np.tile(np.random.uniform(0.5, 2.0, S), (128, 1)).astype(np.float32),
        "offs": striped(np.random.permutation(T)[:S]),
        "offs2": striped(np.random.permutation(T)[:S]),
    }


def reference(tab, w4_words, w4_scales, c, u, b, wgo, offs, offs2):
    tab_ = unpack_table(tab)[:, unstriped(offs)]
    w4_ = unpack_weight(w4_words, w4_scales, "e2m1")
    c_ = mxq(f64(c), 0, "e4m3")
    u_ = mxq(f64(u), 0, "e4m3")
    y = w4_.T @ tab_ + u_.T @ c_
    out = np.zeros((M, T))
    out[:, unstriped(offs2)] = f64(wgo)[0] * (silu(y + f64(b)[:, None]))
    return out

@@ -1,0 +1,168 @@
+from contextlib import ExitStack
+
+import concourse.mybir as mybir
+
+K, M, T, S, L = 1024, 512, 1024, 512, 512
+FLOPS = 2 * (K + L) * M * S
+
+F32 = mybir.dt.float32
+BF16 = mybir.dt.bfloat16
+I32 = mybir.dt.int32
+U32 = mybir.dt.uint32
+U16 = mybir.dt.uint16
+U8 = mybir.dt.uint8
+FP8X4 = mybir.dt.float8_e4m3fn_x4
+FP4X4 = mybir.dt.float4_e2m1fn_x4
+ACT = mybir.ActivationFunctionType
+ALU = mybir.AluOpType
+
+P = 128
+PACK = 4
+PASSES = K // (P * PACK)
+N_TILES = M // P
+WINDOWS = 3
+HALF = S // 2
+
+
+def tile_list_tabscat_d_silu_kernel(tc, tab, w4_words, w4_scales, c, u, b, wgo, offs, offs2, out):
+    nc = tc.nc
+    with ExitStack() as ctx:
+        keep = ctx.enter_context(tc.tile_pool(name="keep", bufs=1))
+        psum = ctx.enter_context(tc.psum_pool(name="psum", bufs=1))
+
+        tab_scales = keep.tile([P, PASSES * T], U8, name="tab_scales", align_bytes=64)
+        w_scales = keep.tile([P, PASSES * M], U8, name="w_scales", align_bytes=64)
+        nc.vector.memset(tab_scales[:, 0:T].bitcast(I32), 0)
+        nc.gpsimd.memset(tab_scales[:, T : 2 * T].bitcast(I32), 0)
+        nc.vector.memset(w_scales[:].bitcast(I32), 0)
+        windows = [keep.tile([P, T], F32, name="window%d" % i) for i in range(WINDOWS)]
+        for window in windows:
+            nc.vector.memset(window[:], 0.0)
+
+        warm_in = keep.tile([P, 1], F32, name="warm_in")
+        warm_out = keep.tile([P, 1], F32, name="warm_out")
+        nc.gpsimd.memset(warm_in[:], 0.0)
+        nc.scalar.activation(warm_out[:], warm_in[:], ACT.Silu)
+
+        gather_list = keep.tile([P, S // 16], U16, name="gather_list")
+        scatter_list = keep.tile([P, S // 16], U16, name="scatter_list")
+        nc.sync.dma_start(gather_list[:], offs)
+        nc.sync.dma_start(scatter_list[:], offs2)
+        bias = keep.tile([P, N_TILES], F32, name="bias")
+        with nc.allow_non_contiguous_dma(reason="one bias value a partition"):
+            nc.sync.dma_start(bias[:], b.rearrange("(m p) -> p m", p=P))
+
+        tab_scale_rows = tab[:, 512 * T :].bitcast(I32).rearrange("a (q r t) -> q r a t", q=4, r=4)
+        for q in range(4):
+            nc.sync.dma_start(
+                tab_scales[32 * q : 32 * q + 4, :].bitcast(I32).rearrange("r (a t) -> r a t", a=PASSES), tab_scale_rows[q]
+            )
+
+        def load_raw(name, src, half):
+            raw = keep.tile([P, PACK, HALF], F32, name=name)
+            nc.sync.dma_start(raw[:], src.rearrange("(p t) w -> p t w", t=PACK)[:, :, half * HALF : (half + 1) * HALF])
+            return raw
+
+        def load_table(a):
+            words = keep.tile([P, T], I32, name="tab_words%d" % a)
+            nc.sync.dma_start(words[:], tab[a, 0 : 512 * T].bitcast(I32).rearrange("(p t) -> p t", p=P))
+            return words
+
+        tab_words0 = load_table(0)
+        c_raw0 = load_raw("c_raw0", c, 0)
+        tab_words1 = load_table(1)
+        u_raw0 = load_raw("u_raw0", u, 0)
+        w_words = keep.tile([P, PASSES, 2 * M], U8, name="w_words", align_bytes=64)
+        nc.sync.dma_start(w_words[:].bitcast(I32), w4_words.bitcast(I32).rearrange("a p n -> p a n"))
+        w_scale_rows = w4_scales.bitcast(I32).rearrange("a (q r) n -> q r a n", r=4)
+        for q in range(4):
+            nc.sync.dma_start(
+                w_scales[32 * q : 32 * q + 4, :].bitcast(I32).rearrange("r (a n) -> r a n", a=PASSES), w_scale_rows[q]
+            )
+        weight = keep.tile([P, S], F32, name="weight")
+        nc.sync.dma_start(weight[:], wgo)
+        c_raw1 = load_raw("c_raw1", c, 1)
+        u_raw1 = load_raw("u_raw1", u, 1)
+
+        def quantize(name, raw, tag):
+            grouped = keep.tile([P, HALF, PACK], BF16, name=name + "_grouped", tag=tag, align_bytes=64)
+            nc.scalar.copy(
+                grouped[:].rearrange("p (w i) t -> p w t i", i=4), raw[:].rearrange("p t (w i) -> p w t i", i=4)
+            )
+            return grouped
+
+        def quantize_into(grouped, codes, scales):
+            nc.vector.quantize_mx(
+                out=codes.bitcast(FP8X4), scales=scales, in_=grouped[:].rearrange("p w t -> p (w t)")
+            )
+
+        picked_scales = [keep.tile([P, S], U8, name="picked_scales%d" % a, align_bytes=64) for a in range(PASSES)]
+        for a in range(PASSES):
+            nc.vector.tensor_copy(picked_scales[a][:], tab_scales[:, a * T : (a + 1) * T].indirect(gather_list[:]))
+
+        picked0 = keep.tile([P, S], U32, name="picked0", align_bytes=64)
+        nc.vector.tensor_copy(picked0[:], tab_words0[:].bitcast(U32).indirect(gather_list[:]))
+
+        def gather_second_pass(h, tag):
+            picked = keep.tile([P, HALF], U32, name="picked1_%d" % h, tag=tag, align_bytes=64)
+            offsets = gather_list[:, h * HALF // 16 : (h + 1) * HALF // 16]
+            nc.vector.tensor_copy(picked[:], tab_words1[:].bitcast(U32).indirect(offsets))
+            return picked
+
+        c_codes = keep.tile([P, S], U32, name="c_codes", align_bytes=64)
+        c_scales = keep.tile([P, S], U8, name="c_scales", align_bytes=64)
+        u_codes = keep.tile([P, M], U32, name="u_codes", align_bytes=64)
+        u_scales = keep.tile([P, M], U8, name="u_scales", align_bytes=64)
+
+        picked1 = [gather_second_pass(0, "picked1_0")]
+        quantize_into(quantize("c0", c_raw0, "c0"), c_codes[:, 0:HALF], c_scales[:, 0:HALF])
+        quantize_into(quantize("u0", u_raw0, "u0"), u_codes[:, 0:HALF], u_scales[:, 0:HALF])
+        picked1.append(gather_second_pass(1, "u0"))
+
+        def unit(m, first, width, dense_first):
+            rows = slice(m * P, (m + 1) * P)
+            acc = psum.tile([P, width], F32, name="acc%d_%d" % (m, first))
+            passes = []
+            for a in range(PASSES):
+                step = S if (a == 0 and width == S) else P
+                for j in range(first, first + width, step):
+                    words = picked0[:, j : j + step] if a == 0 else picked1[j // HALF][:, j % HALF : j % HALF + step]
+                    passes.append(
+                        dict(
+                            out=acc[:, j - first : j - first + step],
+                            lhsT=w_words[:, a, 2 * m * P : 2 * (m + 1) * P].bitcast(FP4X4),
+                            lhsT_scale=w_scales[:, a * M + m * P : a * M + (m + 1) * P],
+                            rhs=words.bitcast(FP8X4),
+                            rhs_scale=picked_scales[a][:, j : j + step],
+                        )
+                    )
+            dense = dict(
+                out=acc[:],
+                lhsT=u_codes[:, rows].bitcast(FP8X4),
+                lhsT_scale=u_scales[:, rows],
+                rhs=c_codes[:, first : first + width].bitcast(FP8X4),
+                rhs_scale=c_scales[:, first : first + width],
+            )
+            passes = [dense] + passes if dense_first else passes + [dense]
+            for i, operands in enumerate(passes):
+                nc.tensor.matmul_mx(start=(i == 0), stop=(i == len(passes) - 1), **operands)
+            values = keep.tile([P, width], F32, name="values%d_%d" % (m, first))
+            nc.scalar.activation(values[:], acc[:], ACT.Silu, bias=bias[:, m : m + 1])
+            return values
+
+        def place(m, first, width, values):
+            window = windows[m % WINDOWS]
+            offsets = scatter_list[:, first // 16 : (first + width) // 16]
+            nc.vector.tensor_tensor(window[:].indirect(offsets), values[:], weight[:, first : first + width], ALU.mult)
+            if first + width == S:
+                nc.sync.dma_start(out[m * P : (m + 1) * P, :], window[:])
+
+        v = unit(0, 0, HALF, False)
+        place(0, 0, HALF, v)
+        quantize_into(quantize("c1", c_raw1, "c1"), c_codes[:, HALF:S], c_scales[:, HALF:S])
+        place(1, 0, HALF, unit(1, 0, HALF, True))
+        quantize_into(quantize("u1", u_raw1, "u1"), u_codes[:, HALF:M], u_scales[:, HALF:M])
+        for m in range(2):
+            place(m, HALF, HALF, unit(m, HALF, HALF, True))
+        for m in range(2, N_TILES):
+            place(m, 0, S, unit(m, 0, S, True))

@@ -1,6 +1,7 @@
 from contextlib import ExitStack
 
 import concourse.mybir as mybir
+from concourse.masks import make_identity
 
 K, M, T, S, L = 1024, 512, 1024, 512, 512
 FLOPS = 2 * (K + L) * M * S
@@ -20,8 +21,8 @@ P = 128
 PACK = 4
 PASSES = K // (P * PACK)
 N_TILES = M // P
-WINDOWS = 3
 HALF = S // 2
+CLEAR_SPLIT = 1536
 
 
 def tile_list_tabscat_d_silu_kernel(tc, tab, w4_words, w4_scales, c, u, b, wgo, offs, offs2, out):
@@ -32,10 +33,12 @@ def tile_list_tabscat_d_silu_kernel(tc, tab, w4_words, w4_scales, c, u, b, wgo, 
 
         tab_scales = keep.tile([P, PASSES * T], U8, name="tab_scales", align_bytes=64)
         w_scales = keep.tile([P, PASSES * M], U8, name="w_scales", align_bytes=64)
-        nc.vector.memset(tab_scales[:, 0:T].bitcast(I32), 0)
-        nc.gpsimd.memset(tab_scales[:, T : 2 * T].bitcast(I32), 0)
+        bias_rows = keep.tile([P, P], F32, name="bias_rows")
+        nc.gpsimd.memset(bias_rows[:], 0.0)
+        nc.vector.memset(tab_scales[:, 0:CLEAR_SPLIT].bitcast(I32), 0)
+        nc.gpsimd.memset(tab_scales[:, CLEAR_SPLIT : PASSES * T].bitcast(I32), 0)
         nc.vector.memset(w_scales[:].bitcast(I32), 0)
-        windows = [keep.tile([P, T], F32, name="window%d" % i) for i in range(WINDOWS)]
+        windows = [keep.tile([P, T], F32, name="window%d" % m) for m in range(N_TILES)]
         for window in windows:
             nc.vector.memset(window[:], 0.0)
 
@@ -43,24 +46,25 @@ def tile_list_tabscat_d_silu_kernel(tc, tab, w4_words, w4_scales, c, u, b, wgo, 
         warm_out = keep.tile([P, 1], F32, name="warm_out")
         nc.gpsimd.memset(warm_in[:], 0.0)
         nc.scalar.activation(warm_out[:], warm_in[:], ACT.Silu)
+        identity = keep.tile([P, P], F32, name="identity")
+        make_identity(nc, identity[:])
 
         gather_list = keep.tile([P, S // 16], U16, name="gather_list")
         scatter_list = keep.tile([P, S // 16], U16, name="scatter_list")
         nc.sync.dma_start(gather_list[:], offs)
         nc.sync.dma_start(scatter_list[:], offs2)
-        bias = keep.tile([P, N_TILES], F32, name="bias")
-        with nc.allow_non_contiguous_dma(reason="one bias value a partition"):
-            nc.sync.dma_start(bias[:], b.rearrange("(m p) -> p m", p=P))
+        nc.sync.dma_start(bias_rows[0:N_TILES, :], b.rearrange("(m p) -> m p", p=P))
 
         tab_scale_rows = tab[:, 512 * T :].bitcast(I32).rearrange("a (q r t) -> q r a t", q=4, r=4)
         for q in range(4):
             nc.sync.dma_start(
-                tab_scales[32 * q : 32 * q + 4, :].bitcast(I32).rearrange("r (a t) -> r a t", a=PASSES), tab_scale_rows[q]
+                tab_scales[32 * q : 32 * q + 4, :].bitcast(I32).rearrange("r (a t) -> r a t", a=PASSES),
+                tab_scale_rows[q],
             )
 
-        def load_raw(name, src, half):
-            raw = keep.tile([P, PACK, HALF], F32, name=name)
-            nc.sync.dma_start(raw[:], src.rearrange("(p t) w -> p t w", t=PACK)[:, :, half * HALF : (half + 1) * HALF])
+        def load_raw(name, src, first, width):
+            raw = keep.tile([P, PACK, width], F32, name=name, tag=name)
+            nc.sync.dma_start(raw[:], src.rearrange("(p t) w -> p t w", t=PACK)[:, :, first : first + width])
             return raw
 
         def load_table(a):
@@ -69,9 +73,9 @@ def tile_list_tabscat_d_silu_kernel(tc, tab, w4_words, w4_scales, c, u, b, wgo, 
             return words
 
         tab_words0 = load_table(0)
-        c_raw0 = load_raw("c_raw0", c, 0)
+        c_raw0 = load_raw("c_raw0", c, 0, HALF)
+        u_raw01 = load_raw("u_raw01", u, 0, 2 * P)
         tab_words1 = load_table(1)
-        u_raw0 = load_raw("u_raw0", u, 0)
         w_words = keep.tile([P, PASSES, 2 * M], U8, name="w_words", align_bytes=64)
         nc.sync.dma_start(w_words[:].bitcast(I32), w4_words.bitcast(I32).rearrange("a p n -> p a n"))
         w_scale_rows = w4_scales.bitcast(I32).rearrange("a (q r) n -> q r a n", r=4)
@@ -81,88 +85,98 @@ def tile_list_tabscat_d_silu_kernel(tc, tab, w4_words, w4_scales, c, u, b, wgo, 
             )
         weight = keep.tile([P, S], F32, name="weight")
         nc.sync.dma_start(weight[:], wgo)
-        c_raw1 = load_raw("c_raw1", c, 1)
-        u_raw1 = load_raw("u_raw1", u, 1)
+        u_raw2 = load_raw("u_raw2", u, 2 * P, P)
+        u_raw3 = load_raw("u_raw3", u, 3 * P, P)
+        c_raw1 = load_raw("c_raw1", c, HALF, HALF)
+        u_raw = [u_raw01[:, :, 0:P], u_raw01[:, :, P : 2 * P], u_raw2[:], u_raw3[:]]
+        reused = {(1, 0): "u_raw2", (2, 0): "u_raw3", (3, 0): "c_raw1"}
 
-        def quantize(name, raw, tag):
-            grouped = keep.tile([P, HALF, PACK], BF16, name=name + "_grouped", tag=tag, align_bytes=64)
-            nc.scalar.copy(
-                grouped[:].rearrange("p (w i) t -> p w t i", i=4), raw[:].rearrange("p t (w i) -> p w t i", i=4)
-            )
-            return grouped
+        bias_turned = psum.tile([P, P], F32, name="bias_turned")
+        nc.tensor.transpose(bias_turned[:], bias_rows[:], identity[:])
+        bias = keep.tile([P, N_TILES], F32, name="bias")
+        nc.scalar.copy(bias[:], bias_turned[:, 0:N_TILES])
 
-        def quantize_into(grouped, codes, scales):
-            nc.vector.quantize_mx(
-                out=codes.bitcast(FP8X4), scales=scales, in_=grouped[:].rearrange("p w t -> p (w t)")
-            )
+        def interleave(grouped, raw):
+            nc.scalar.copy(grouped.rearrange("p (w i) t -> p w t i", i=4), raw.rearrange("p t (w i) -> p w t i", i=4))
 
-        picked_scales = [keep.tile([P, S], U8, name="picked_scales%d" % a, align_bytes=64) for a in range(PASSES)]
-        for a in range(PASSES):
-            nc.vector.tensor_copy(picked_scales[a][:], tab_scales[:, a * T : (a + 1) * T].indirect(gather_list[:]))
-
-        picked0 = keep.tile([P, S], U32, name="picked0", align_bytes=64)
-        nc.vector.tensor_copy(picked0[:], tab_words0[:].bitcast(U32).indirect(gather_list[:]))
-
-        def gather_second_pass(h, tag):
-            picked = keep.tile([P, HALF], U32, name="picked1_%d" % h, tag=tag, align_bytes=64)
-            offsets = gather_list[:, h * HALF // 16 : (h + 1) * HALF // 16]
-            nc.vector.tensor_copy(picked[:], tab_words1[:].bitcast(U32).indirect(offsets))
-            return picked
+        def quantize(codes, scales, grouped):
+            nc.vector.quantize_mx(out=codes.bitcast(FP8X4), scales=scales, in_=grouped.rearrange("p w t -> p (w t)"))
 
         c_codes = keep.tile([P, S], U32, name="c_codes", align_bytes=64)
         c_scales = keep.tile([P, S], U8, name="c_scales", align_bytes=64)
         u_codes = keep.tile([P, M], U32, name="u_codes", align_bytes=64)
         u_scales = keep.tile([P, M], U8, name="u_scales", align_bytes=64)
 
-        picked1 = [gather_second_pass(0, "picked1_0")]
-        quantize_into(quantize("c0", c_raw0, "c0"), c_codes[:, 0:HALF], c_scales[:, 0:HALF])
-        quantize_into(quantize("u0", u_raw0, "u0"), u_codes[:, 0:HALF], u_scales[:, 0:HALF])
-        picked1.append(gather_second_pass(1, "u0"))
+        def prepare_c(h, raw):
+            grouped = keep.tile([P, HALF, PACK], BF16, name="c_grouped%d" % h, align_bytes=64)
+            for j in range(0, HALF, P):
+                interleave(grouped[:, j : j + P, :], raw[:, :, j : j + P])
+            cols = slice(h * HALF, (h + 1) * HALF)
+            quantize(c_codes[:, cols], c_scales[:, cols], grouped[:])
 
-        def unit(m, first, width, dense_first):
+        def prepare_u(m):
+            grouped = keep.tile([P, P, PACK], BF16, name="u_grouped%d" % m, align_bytes=64)
+            interleave(grouped[:], u_raw[m])
+            cols = slice(m * P, (m + 1) * P)
+            quantize(u_codes[:, cols], u_scales[:, cols], grouped[:])
+
+        picked_scales = [keep.tile([P, S], U8, name="picked_scales%d" % a, align_bytes=64) for a in range(PASSES)]
+        picked_words = [keep.tile([P, S], U32, name="picked_words%d" % a, align_bytes=64) for a in range(PASSES)]
+        nc.vector.tensor_copy(picked_words[0][:], tab_words0[:].bitcast(U32).indirect(gather_list[:]))
+        for a in range(PASSES):
+            nc.vector.tensor_copy(picked_scales[a][:], tab_scales[:, a * T : (a + 1) * T].indirect(gather_list[:]))
+        prepare_c(0, c_raw0)
+        prepare_u(0)
+        for h in range(2):
+            nc.vector.tensor_copy(
+                picked_words[1][:, h * HALF : (h + 1) * HALF],
+                tab_words1[:].bitcast(U32).indirect(gather_list[:, h * HALF // 16 : (h + 1) * HALF // 16]),
+            )
+        prepare_u(1)
+
+        def project(m, h):
             rows = slice(m * P, (m + 1) * P)
-            acc = psum.tile([P, width], F32, name="acc%d_%d" % (m, first))
-            passes = []
-            for a in range(PASSES):
-                step = S if (a == 0 and width == S) else P
-                for j in range(first, first + width, step):
-                    words = picked0[:, j : j + step] if a == 0 else picked1[j // HALF][:, j % HALF : j % HALF + step]
-                    passes.append(
-                        dict(
-                            out=acc[:, j - first : j - first + step],
-                            lhsT=w_words[:, a, 2 * m * P : 2 * (m + 1) * P].bitcast(FP4X4),
-                            lhsT_scale=w_scales[:, a * M + m * P : a * M + (m + 1) * P],
-                            rhs=words.bitcast(FP8X4),
-                            rhs_scale=picked_scales[a][:, j : j + step],
-                        )
-                    )
+            first = h * HALF
+            acc = psum.tile([P, HALF], F32, name="acc", bufs=6)
             dense = dict(
                 out=acc[:],
                 lhsT=u_codes[:, rows].bitcast(FP8X4),
                 lhsT_scale=u_scales[:, rows],
-                rhs=c_codes[:, first : first + width].bitcast(FP8X4),
-                rhs_scale=c_scales[:, first : first + width],
+                rhs=c_codes[:, first : first + HALF].bitcast(FP8X4),
+                rhs_scale=c_scales[:, first : first + HALF],
             )
-            passes = [dense] + passes if dense_first else passes + [dense]
+            looked_up = [
+                dict(
+                    out=acc[:, j : j + P],
+                    lhsT=w_words[:, a, 2 * m * P : 2 * (m + 1) * P].bitcast(FP4X4),
+                    lhsT_scale=w_scales[:, a * M + m * P : a * M + (m + 1) * P],
+                    rhs=picked_words[a][:, first + j : first + j + P].bitcast(FP8X4),
+                    rhs_scale=picked_scales[a][:, first + j : first + j + P],
+                )
+                for a in range(PASSES)
+                for j in range(0, HALF, P)
+            ]
+            passes = looked_up + [dense] if (m, h) == (1, 0) else [dense] + looked_up
             for i, operands in enumerate(passes):
                 nc.tensor.matmul_mx(start=(i == 0), stop=(i == len(passes) - 1), **operands)
-            values = keep.tile([P, width], F32, name="values%d_%d" % (m, first))
+            name = "values%d_%d" % (m, h)
+            values = keep.tile([P, HALF], F32, name=name, tag=reused.get((m, h), name))
             nc.scalar.activation(values[:], acc[:], ACT.Silu, bias=bias[:, m : m + 1])
             return values
 
-        def place(m, first, width, values):
-            window = windows[m % WINDOWS]
-            offsets = scatter_list[:, first // 16 : (first + width) // 16]
-            nc.vector.tensor_tensor(window[:].indirect(offsets), values[:], weight[:, first : first + width], ALU.mult)
-            if first + width == S:
-                nc.sync.dma_start(out[m * P : (m + 1) * P, :], window[:])
+        def place(m, h, values):
+            offsets = scatter_list[:, h * HALF // 16 : (h + 1) * HALF // 16]
+            nc.vector.tensor_tensor(
+                windows[m][:].indirect(offsets), values[:], weight[:, h * HALF : (h + 1) * HALF], ALU.mult
+            )
 
-        v = unit(0, 0, HALF, False)
-        place(0, 0, HALF, v)
-        quantize_into(quantize("c1", c_raw1, "c1"), c_codes[:, HALF:S], c_scales[:, HALF:S])
-        place(1, 0, HALF, unit(1, 0, HALF, True))
-        quantize_into(quantize("u1", u_raw1, "u1"), u_codes[:, HALF:M], u_scales[:, HALF:M])
-        for m in range(2):
-            place(m, HALF, HALF, unit(m, HALF, HALF, True))
-        for m in range(2, N_TILES):
-            place(m, 0, S, unit(m, 0, S, True))
+        for m in range(N_TILES):
+            values = project(m, 0)
+            place(m, 0, values)
+            if m + 2 < N_TILES:
+                prepare_u(m + 2)
+            if m + 2 == N_TILES:
+                prepare_c(1, c_raw1)
+        for m in range(N_TILES):
+            place(m, 1, project(m, 1))
+            nc.sync.dma_start(out[m * P : (m + 1) * P, :], windows[m][:])

@@ -49,19 +49,6 @@ def tile_list_tabscat_d_silu_kernel(tc, tab, w4_words, w4_scales, c, u, b, wgo, 
         identity = keep.tile([P, P], F32, name="identity")
         make_identity(nc, identity[:])
 
-        gather_list = keep.tile([P, S // 16], U16, name="gather_list")
-        scatter_list = keep.tile([P, S // 16], U16, name="scatter_list")
-        nc.sync.dma_start(gather_list[:], offs)
-        nc.sync.dma_start(scatter_list[:], offs2)
-        nc.sync.dma_start(bias_rows[0:N_TILES, :], b.rearrange("(m p) -> m p", p=P))
-
-        tab_scale_rows = tab[:, 512 * T :].bitcast(I32).rearrange("a (q r t) -> q r a t", q=4, r=4)
-        for q in range(4):
-            nc.sync.dma_start(
-                tab_scales[32 * q : 32 * q + 4, :].bitcast(I32).rearrange("r (a t) -> r a t", a=PASSES),
-                tab_scale_rows[q],
-            )
-
         def load_raw(name, src, first, width):
             raw = keep.tile([P, PACK, width], F32, name=name, tag=name)
             nc.sync.dma_start(raw[:], src.rearrange("(p t) w -> p t w", t=PACK)[:, :, first : first + width])
@@ -72,20 +59,40 @@ def tile_list_tabscat_d_silu_kernel(tc, tab, w4_words, w4_scales, c, u, b, wgo, 
             nc.sync.dma_start(words[:], tab[a, 0 : 512 * T].bitcast(I32).rearrange("(p t) -> p t", p=P))
             return words
 
+        def load_w(half):
+            words = keep.tile([P, PASSES, M], U8, name="w_words%d" % half, align_bytes=64)
+            nc.sync.dma_start(
+                words[:].bitcast(I32), w4_words[:, :, half * M : (half + 1) * M].bitcast(I32).rearrange("a p n -> p a n")
+            )
+            return words
+
+        gather_list = keep.tile([P, S // 16], U16, name="gather_list")
+        scatter_list = keep.tile([P, S // 16], U16, name="scatter_list")
+        nc.sync.dma_start(gather_list[:], offs)
         tab_words0 = load_table(0)
+        nc.sync.dma_start(scatter_list[:], offs2)
+        nc.sync.dma_start(bias_rows[0:N_TILES, :], b.rearrange("(m p) -> m p", p=P))
+
+        tab_scale_rows = tab[:, 512 * T :].bitcast(I32).rearrange("a (q r t) -> q r a t", q=4, r=4)
+        for q in range(4):
+            nc.sync.dma_start(
+                tab_scales[32 * q : 32 * q + 4, :].bitcast(I32).rearrange("r (a t) -> r a t", a=PASSES),
+                tab_scale_rows[q],
+            )
+
         c_raw0 = load_raw("c_raw0", c, 0, HALF)
         u_raw01 = load_raw("u_raw01", u, 0, 2 * P)
-        tab_words1 = load_table(1)
-        w_words = keep.tile([P, PASSES, 2 * M], U8, name="w_words", align_bytes=64)
-        nc.sync.dma_start(w_words[:].bitcast(I32), w4_words.bitcast(I32).rearrange("a p n -> p a n"))
         w_scale_rows = w4_scales.bitcast(I32).rearrange("a (q r) n -> q r a n", r=4)
         for q in range(4):
             nc.sync.dma_start(
                 w_scales[32 * q : 32 * q + 4, :].bitcast(I32).rearrange("r (a n) -> r a n", a=PASSES), w_scale_rows[q]
             )
+        tab_words1 = load_table(1)
+        w_words = [load_w(0)]
         weight = keep.tile([P, S], F32, name="weight")
         nc.sync.dma_start(weight[:], wgo)
         u_raw2 = load_raw("u_raw2", u, 2 * P, P)
+        w_words.append(load_w(1))
         u_raw3 = load_raw("u_raw3", u, 3 * P, P)
         c_raw1 = load_raw("c_raw1", c, HALF, HALF)
         u_raw = [u_raw01[:, :, 0:P], u_raw01[:, :, P : 2 * P], u_raw2[:], u_raw3[:]]
@@ -137,7 +144,7 @@ def tile_list_tabscat_d_silu_kernel(tc, tab, w4_words, w4_scales, c, u, b, wgo, 
         def project(m, h):
             rows = slice(m * P, (m + 1) * P)
             first = h * HALF
-            acc = psum.tile([P, HALF], F32, name="acc", bufs=6)
+            acc = psum.tile([P, HALF], F32, name="acc", bufs=7)
             dense = dict(
                 out=acc[:],
                 lhsT=u_codes[:, rows].bitcast(FP8X4),
@@ -148,7 +155,7 @@ def tile_list_tabscat_d_silu_kernel(tc, tab, w4_words, w4_scales, c, u, b, wgo, 
             looked_up = [
                 dict(
                     out=acc[:, j : j + P],
-                    lhsT=w_words[:, a, 2 * m * P : 2 * (m + 1) * P].bitcast(FP4X4),
+                    lhsT=w_words[m // 2][:, a, 2 * (m % 2) * P : 2 * (m % 2 + 1) * P].bitcast(FP4X4),
                     lhsT_scale=w_scales[:, a * M + m * P : a * M + (m + 1) * P],
                     rhs=picked_words[a][:, first + j : first + j + P].bitcast(FP8X4),
                     rhs_scale=picked_scales[a][:, first + j : first + j + P],
@@ -156,7 +163,7 @@ def tile_list_tabscat_d_silu_kernel(tc, tab, w4_words, w4_scales, c, u, b, wgo, 
                 for a in range(PASSES)
                 for j in range(0, HALF, P)
             ]
-            passes = looked_up + [dense] if (m, h) == (1, 0) else [dense] + looked_up
+            passes = [dense] + looked_up if (m, h) == (0, 0) else looked_up + [dense]
             for i, operands in enumerate(passes):
                 nc.tensor.matmul_mx(start=(i == 0), stop=(i == len(passes) - 1), **operands)
             name = "values%d_%d" % (m, h)

@@ -42,10 +42,6 @@ def tile_list_tabscat_d_silu_kernel(tc, tab, w4_words, w4_scales, c, u, b, wgo, 
         for window in windows:
             nc.vector.memset(window[:], 0.0)
 
-        warm_in = keep.tile([P, 1], F32, name="warm_in")
-        warm_out = keep.tile([P, 1], F32, name="warm_out")
-        nc.gpsimd.memset(warm_in[:], 0.0)
-        nc.scalar.activation(warm_out[:], warm_in[:], ACT.Silu)
         identity = keep.tile([P, P], F32, name="identity")
         make_identity(nc, identity[:])
 

from contextlib import ExitStack

import concourse.mybir as mybir
from concourse.masks import make_identity

K, M, T, S, L = 1024, 512, 1024, 512, 512
FLOPS = 2 * (K + L) * M * S

F32 = mybir.dt.float32
BF16 = mybir.dt.bfloat16
I32 = mybir.dt.int32
U32 = mybir.dt.uint32
U16 = mybir.dt.uint16
U8 = mybir.dt.uint8
FP8X4 = mybir.dt.float8_e4m3fn_x4
FP4X4 = mybir.dt.float4_e2m1fn_x4
ACT = mybir.ActivationFunctionType
ALU = mybir.AluOpType

P = 128
PACK = 4
PASSES = K // (P * PACK)
N_TILES = M // P
HALF = S // 2
CLEAR_SPLIT = 1536


def tile_list_tabscat_d_silu_kernel(tc, tab, w4_words, w4_scales, c, u, b, wgo, offs, offs2, out):
    nc = tc.nc
    with ExitStack() as ctx:
        keep = ctx.enter_context(tc.tile_pool(name="keep", bufs=1))
        psum = ctx.enter_context(tc.psum_pool(name="psum", bufs=1))

        tab_scales = keep.tile([P, PASSES * T], U8, name="tab_scales", align_bytes=64)
        w_scales = keep.tile([P, PASSES * M], U8, name="w_scales", align_bytes=64)
        bias_rows = keep.tile([P, P], F32, name="bias_rows")
        nc.gpsimd.memset(bias_rows[:], 0.0)
        nc.vector.memset(tab_scales[:, 0:CLEAR_SPLIT].bitcast(I32), 0)
        nc.gpsimd.memset(tab_scales[:, CLEAR_SPLIT : PASSES * T].bitcast(I32), 0)
        nc.vector.memset(w_scales[:].bitcast(I32), 0)
        windows = [keep.tile([P, T], F32, name="window%d" % m) for m in range(N_TILES)]
        for window in windows:
            nc.vector.memset(window[:], 0.0)

        identity = keep.tile([P, P], F32, name="identity")
        make_identity(nc, identity[:])

        def load_raw(name, src, first, width):
            raw = keep.tile([P, PACK, width], F32, name=name, tag=name)
            nc.sync.dma_start(raw[:], src.rearrange("(p t) w -> p t w", t=PACK)[:, :, first : first + width])
            return raw

        def load_table(a):
            words = keep.tile([P, T], I32, name="tab_words%d" % a)
            nc.sync.dma_start(words[:], tab[a, 0 : 512 * T].bitcast(I32).rearrange("(p t) -> p t", p=P))
            return words

        def load_w(half):
            words = keep.tile([P, PASSES, M], U8, name="w_words%d" % half, align_bytes=64)
            nc.sync.dma_start(
                words[:].bitcast(I32), w4_words[:, :, half * M : (half + 1) * M].bitcast(I32).rearrange("a p n -> p a n")
            )
            return words

        gather_list = keep.tile([P, S // 16], U16, name="gather_list")
        scatter_list = keep.tile([P, S // 16], U16, name="scatter_list")
        nc.sync.dma_start(gather_list[:], offs)
        tab_words0 = load_table(0)
        nc.sync.dma_start(scatter_list[:], offs2)
        nc.sync.dma_start(bias_rows[0:N_TILES, :], b.rearrange("(m p) -> m p", p=P))

        tab_scale_rows = tab[:, 512 * T :].bitcast(I32).rearrange("a (q r t) -> q r a t", q=4, r=4)
        for q in range(4):
            nc.sync.dma_start(
                tab_scales[32 * q : 32 * q + 4, :].bitcast(I32).rearrange("r (a t) -> r a t", a=PASSES),
                tab_scale_rows[q],
            )

        c_raw0 = load_raw("c_raw0", c, 0, HALF)
        u_raw01 = load_raw("u_raw01", u, 0, 2 * P)
        w_scale_rows = w4_scales.bitcast(I32).rearrange("a (q r) n -> q r a n", r=4)
        for q in range(4):
            nc.sync.dma_start(
                w_scales[32 * q : 32 * q + 4, :].bitcast(I32).rearrange("r (a n) -> r a n", a=PASSES), w_scale_rows[q]
            )
        tab_words1 = load_table(1)
        w_words = [load_w(0)]
        weight = keep.tile([P, S], F32, name="weight")
        nc.sync.dma_start(weight[:], wgo)
        u_raw2 = load_raw("u_raw2", u, 2 * P, P)
        w_words.append(load_w(1))
        u_raw3 = load_raw("u_raw3", u, 3 * P, P)
        c_raw1 = load_raw("c_raw1", c, HALF, HALF)
        u_raw = [u_raw01[:, :, 0:P], u_raw01[:, :, P : 2 * P], u_raw2[:], u_raw3[:]]
        reused = {(1, 0): "u_raw2", (2, 0): "u_raw3", (3, 0): "c_raw1"}

        bias_turned = psum.tile([P, P], F32, name="bias_turned")
        nc.tensor.transpose(bias_turned[:], bias_rows[:], identity[:])
        bias = keep.tile([P, N_TILES], F32, name="bias")
        nc.scalar.copy(bias[:], bias_turned[:, 0:N_TILES])

        def interleave(grouped, raw):
            nc.scalar.copy(grouped.rearrange("p (w i) t -> p w t i", i=4), raw.rearrange("p t (w i) -> p w t i", i=4))

        def quantize(codes, scales, grouped):
            nc.vector.quantize_mx(out=codes.bitcast(FP8X4), scales=scales, in_=grouped.rearrange("p w t -> p (w t)"))

        c_codes = keep.tile([P, S], U32, name="c_codes", align_bytes=64)
        c_scales = keep.tile([P, S], U8, name="c_scales", align_bytes=64)
        u_codes = keep.tile([P, M], U32, name="u_codes", align_bytes=64)
        u_scales = keep.tile([P, M], U8, name="u_scales", align_bytes=64)

        def prepare_c(h, raw):
            grouped = keep.tile([P, HALF, PACK], BF16, name="c_grouped%d" % h, align_bytes=64)
            for j in range(0, HALF, P):
                interleave(grouped[:, j : j + P, :], raw[:, :, j : j + P])
            cols = slice(h * HALF, (h + 1) * HALF)
            quantize(c_codes[:, cols], c_scales[:, cols], grouped[:])

        def prepare_u(m):
            grouped = keep.tile([P, P, PACK], BF16, name="u_grouped%d" % m, align_bytes=64)
            interleave(grouped[:], u_raw[m])
            cols = slice(m * P, (m + 1) * P)
            quantize(u_codes[:, cols], u_scales[:, cols], grouped[:])

        picked_scales = [keep.tile([P, S], U8, name="picked_scales%d" % a, align_bytes=64) for a in range(PASSES)]
        picked_words = [keep.tile([P, S], U32, name="picked_words%d" % a, align_bytes=64) for a in range(PASSES)]
        nc.vector.tensor_copy(picked_words[0][:], tab_words0[:].bitcast(U32).indirect(gather_list[:]))
        for a in range(PASSES):
            nc.vector.tensor_copy(picked_scales[a][:], tab_scales[:, a * T : (a + 1) * T].indirect(gather_list[:]))
        prepare_c(0, c_raw0)
        prepare_u(0)
        for h in range(2):
            nc.vector.tensor_copy(
                picked_words[1][:, h * HALF : (h + 1) * HALF],
                tab_words1[:].bitcast(U32).indirect(gather_list[:, h * HALF // 16 : (h + 1) * HALF // 16]),
            )
        prepare_u(1)

        def project(m, h):
            rows = slice(m * P, (m + 1) * P)
            first = h * HALF
            acc = psum.tile([P, HALF], F32, name="acc", bufs=7)
            dense = dict(
                out=acc[:],
                lhsT=u_codes[:, rows].bitcast(FP8X4),
                lhsT_scale=u_scales[:, rows],
                rhs=c_codes[:, first : first + HALF].bitcast(FP8X4),
                rhs_scale=c_scales[:, first : first + HALF],
            )
            looked_up = [
                dict(
                    out=acc[:, j : j + P],
                    lhsT=w_words[m // 2][:, a, 2 * (m % 2) * P : 2 * (m % 2 + 1) * P].bitcast(FP4X4),
                    lhsT_scale=w_scales[:, a * M + m * P : a * M + (m + 1) * P],
                    rhs=picked_words[a][:, first + j : first + j + P].bitcast(FP8X4),
                    rhs_scale=picked_scales[a][:, first + j : first + j + P],
                )
                for a in range(PASSES)
                for j in range(0, HALF, P)
            ]
            passes = [dense] + looked_up if (m, h) == (0, 0) else looked_up + [dense]
            for i, operands in enumerate(passes):
                nc.tensor.matmul_mx(start=(i == 0), stop=(i == len(passes) - 1), **operands)
            name = "values%d_%d" % (m, h)
            values = keep.tile([P, HALF], F32, name=name, tag=reused.get((m, h), name))
            nc.scalar.activation(values[:], acc[:], ACT.Silu, bias=bias[:, m : m + 1])
            return values

        def place(m, h, values):
            offsets = scatter_list[:, h * HALF // 16 : (h + 1) * HALF // 16]
            nc.vector.tensor_tensor(
                windows[m][:].indirect(offsets), values[:], weight[:, h * HALF : (h + 1) * HALF], ALU.mult
            )

        for m in range(N_TILES):
            values = project(m, 0)
            place(m, 0, values)
            if m + 2 < N_TILES:
                prepare_u(m + 2)
            if m + 2 == N_TILES:
                prepare_c(1, c_raw1)
        for m in range(N_TILES):
            place(m, 1, project(m, 1))
            nc.sync.dma_start(out[m * P : (m + 1) * P, :], windows[m][:])
